import numpy as np
import ml_dtypes


def mxq(x, axis, fmt="e4m3"):
    dtype, down = {"e4m3": (ml_dtypes.float8_e4m3fn, 7), "e5m2": (ml_dtypes.float8_e5m2, 14)}[fmt]
    v = np.moveaxis(np.asarray(x, np.float32).astype(ml_dtypes.bfloat16).astype(np.float64), axis, -1)
    blocks = v.reshape(v.shape[:-1] + (-1, 32))
    amax = np.abs(blocks).max(-1, keepdims=True)
    byte = np.maximum(np.where(amax > 0, np.frexp(amax)[1] - 1 + 127, 0) - down, 1)
    scale = np.exp2(byte - 127.0)
    codes = (blocks / scale).astype(np.float32).astype(dtype).astype(np.float64)
    return np.moveaxis((codes * scale).reshape(v.shape), -1, axis)


WIDE = False


def mx_kscale(k):
    if not WIDE:
        return np.ones(k)
    levels = np.array([10, -10, 5, -5, 0])
    if k % 512:
        return np.exp2(np.random.permutation(np.resize(levels, k // 32))).repeat(32)
    a = np.empty((k // 512, 16))
    for p in range(k // 512):
        a[p, :8] = np.random.permutation(np.resize(levels, 8))
        for g in range(8):
            far = levels[np.abs(levels - a[p, g]) >= 10]
            a[p, g + 8] = far[np.random.randint(len(far))]
    return np.exp2(a.ravel()).repeat(32)


def f64(x):
    return np.asarray(x).astype(np.float64)


def striped(idx):
    return np.tile(idx.reshape(-1, 16).T, (8, 1)).astype(np.uint16)


def unstriped(offs):
    return offs[:16].T.reshape(-1).astype(np.int64)


E2M1 = np.array([0.0, 0.5, 1.0, 1.5, 2.0, 3.0, 4.0, 6.0, -0.0, -0.5, -1.0, -1.5, -2.0, -3.0, -4.0, -6.0])


def pack_weight(w, fmt):
    k, n = w.shape
    w = f64(np.asarray(w, np.float32).astype(ml_dtypes.bfloat16)).reshape(k // 32, 32, n)
    amax = np.abs(w).max(1)
    if fmt == "e4m3":
        byte = np.frexp(amax)[1] - 1 + 127 - 7
    else:
        mant, ex = np.frexp(amax / 6.0)
        byte = np.where(mant > 0.5, ex, ex - 1) + 127
    byte = np.clip(np.where(amax > 0, byte, 1), 1, 254)
    scaled = (w * np.exp2(127.0 - byte)[:, None, :]).reshape(k, n).astype(np.float32)
    by_word = np.ascontiguousarray(scaled.reshape(k // 512, 128, 4, n).transpose(0, 1, 3, 2))
    if fmt == "e4m3":
        words = by_word.astype(ml_dtypes.float8_e4m3fn).view(np.uint8)
    else:
        c = by_word.astype(ml_dtypes.float4_e2m1fn).view(np.uint8) & 0xF
        words = (c[..., 0::2] | (c[..., 1::2] << 4)).reshape(k // 512, 128, 2 * n)
    return np.ascontiguousarray(words), np.ascontiguousarray(byte.astype(np.uint8).reshape(k // 512, 16, n))


def unpack_weight(words, scales, fmt):
    g, _, n = scales.shape
    words = np.ascontiguousarray(words).reshape(g, 128, n, -1)
    if fmt == "e4m3":
        vals = words.view(ml_dtypes.float8_e4m3fn).astype(np.float64)
    else:
        nib = np.empty((g, 128, n, 4), np.uint8)
        nib[..., 0::2] = words & 0xF
        nib[..., 1::2] = words >> 4
        vals = E2M1[nib]
    vals = vals * np.repeat(np.exp2(scales.astype(np.float64) - 127.0), 8, axis=1)[..., None]
    return vals.transpose(0, 1, 3, 2).reshape(g * 512, n)


def gelu(v):
    return 0.5 * v * (1.0 + np.tanh(np.sqrt(2.0 / np.pi) * (v + 0.044715 * v**3)))


def bf(x):
    return np.asarray(x, np.float32).astype(ml_dtypes.bfloat16)


def planes(Y):
    n, m = Y.shape
    b = f64(bf(Y)).reshape(n // 32, 32, m)
    amax = np.abs(b).max(1)
    byte = np.clip(np.where(amax > 0, np.frexp(amax)[1] - 1 + 127 - 7, 1), 1, 254)
    codes = (b * np.exp2(127.0 - byte)[:, None, :]).reshape(n, m).astype(np.float32).astype(ml_dtypes.float8_e4m3fn).view(np.uint8)
    words = codes.reshape(n // 512, 128, 4, m).transpose(0, 1, 3, 2)
    return np.ascontiguousarray(words), np.ascontiguousarray(byte.astype(np.uint8).reshape(n // 512, 16, m))


K, K3, T, T3, S, H, N = 1024, 512, 2048, 1024, 512, 1024, 512

def setup_inputs():
    n = np.random.standard_normal
    s = mx_kscale(K)[:, None]
    s3 = mx_kscale(K3)[:, None]
    u = mx_kscale(H)[:, None]
    tab_words, tab_scales = pack_weight(n((K, T)) * s, "e4m3")
    tab2_words, tab2_scales = pack_weight(n((K, T)) * s, "e4m3")
    tab3_words, tab3_scales = pack_weight(n((K3, T3)) * s3, "e2m1")
    w2_words, w2_scales = pack_weight(n((K, H)) / np.sqrt(K) / s, "e2m1")
    w3_words, w3_scales = pack_weight(0.8 * n((K3, H)) / np.sqrt(K3) / s3, "e4m3")
    return {
        "tab_words": tab_words, "tab_scales": tab_scales,
        "tab2_words": tab2_words, "tab2_scales": tab2_scales,
        "tab3_words": tab3_words, "tab3_scales": tab3_scales,
        "offs": striped(np.random.permutation(T)[:S]),
        "offs2": striped(np.random.permutation(T)[:S]),
        "offs3": striped(np.random.permutation(T3)[:S]),
        "w1": (n((K, H)) / np.sqrt(K) / s).astype(np.float32),
        "w2_words": w2_words, "w2_scales": w2_scales,
        "w3_words": w3_words, "w3_scales": w3_scales,
        "gain": (np.exp(0.3 * n(H)) * u[:, 0]).astype(np.float32),
        "w4": (n((H, N)) / np.sqrt(H) * np.exp(0.8 * n(N)) / u).astype(np.float32),
    }

def reference(tab_words, tab_scales, tab2_words, tab2_scales, tab3_words, tab3_scales, offs, offs2, offs3, w1, w2_words, w2_scales, w3_words, w3_scales, gain, w4):
    v = unpack_weight(tab_words, tab_scales, "e4m3")[:, unstriped(offs)]
    v2 = unpack_weight(tab2_words, tab2_scales, "e4m3")[:, unstriped(offs2)]
    v3 = unpack_weight(tab3_words, tab3_scales, "e2m1")[:, unstriped(offs3)]
    a = mxq(f64(w1), 0, "e4m3").T @ v
    b = unpack_weight(w2_words, w2_scales, "e2m1").T @ v2
    f = unpack_weight(w3_words, w3_scales, "e4m3").T @ v3
    x1 = a + f
    x2 = b + f
    e1 = 0.5 * x1 * (1 + np.tanh(np.sqrt(2 / np.pi) * (x1 + 0.044715 * x1 ** 3)))
    e2 = 0.5 * x2 * (1 + np.tanh(np.sqrt(2 / np.pi) * (x2 + 0.044715 * x2 ** 3)))
    h = f64(gain)[:, None] * (e1 - e2)
    y = mxq(f64(w4), 0, "e4m3").T @ mxq(h, 0, "e4m3")
    words, scales = planes(y)
    return y, words, scales

@@ -1,0 +1,308 @@
+from contextlib import ExitStack
+
+import concourse.mybir as mybir
+
+K, K3, T, T3, S, H, N = 1024, 512, 2048, 1024, 512, 1024, 512
+FLOPS = 2 * S * (2 * K * H + K3 * H + H * N)
+
+F32 = mybir.dt.float32
+BF16 = mybir.dt.bfloat16
+I32 = mybir.dt.int32
+U32 = mybir.dt.uint32
+U16 = mybir.dt.uint16
+U8 = mybir.dt.uint8
+FP8X4 = mybir.dt.float8_e4m3fn_x4
+FP4X4 = mybir.dt.float4_e2m1fn_x4
+GELU = mybir.ActivationFunctionType.Gelu_apprx_tanh
+COPY = mybir.ActivationFunctionType.Copy
+ADD = mybir.AluOpType.add
+MULT = mybir.AluOpType.mult
+SUBTRACT = mybir.AluOpType.subtract
+
+P = 128
+G = 512
+TAB_ROW = 8
+
+
+def tile_list_lacrosse_matchup_features_kernel(
+    tc, tab_words, tab_scales, tab2_words, tab2_scales, tab3_words, tab3_scales, offs, offs2, offs3,
+    w1, w2_words, w2_scales, w3_words, w3_scales, gain, w4, out_0, out_1, out_2,
+):
+    nc = tc.nc
+    with ExitStack() as ctx:
+        lists = ctx.enter_context(tc.tile_pool(name="lists", bufs=1))
+        sb = ctx.enter_context(tc.tile_pool(name="sb", bufs=1))
+        ps = ctx.enter_context(tc.psum_pool(name="ps", bufs=1))
+
+        def sbuf(name, shape, dtype, tag=""):
+            return sb.tile(shape, dtype, name=name, tag=tag or name, align_bytes=64)
+
+        def bank(tag, name):
+            return ps.tile([P, S], F32, name=name, tag=tag)
+
+        idx = lists.tile([P, S // 16], U16, name="idx")
+        idx2 = lists.tile([P, S // 16], U16, name="idx2")
+        idx3 = lists.tile([P, S // 16], U16, name="idx3")
+
+        t3s = sbuf("t3s", [P, T3], U8)
+        w3s_raw = sbuf("w3s_raw", [P, H], U8)
+        w2s_raw = sbuf("w2s_raw", [P, 2, H], U8)
+        t2s = sbuf("t2s", [P, 2, T], U8)
+        t1s = sbuf("t1s", [P, T], U8)
+        for plane in (t3s[:], w3s_raw[:], w2s_raw[:].rearrange("p a c -> p (a c)")):
+            nc.gpsimd.memset(plane.bitcast(I32), 0)
+        for plane in (t2s[:].rearrange("p a c -> p (a c)"), t1s[:]):
+            nc.vector.memset(plane.bitcast(I32), 0)
+
+        t3w = sbuf("t3w", [P, T3], U16)
+        w3w_raw = sbuf("w3w_raw", [P, H], I32)
+        w2w_raw = sbuf("w2w_raw", [P, 2, H // 2], I32)
+        t2w = [sbuf("t2w%d" % a, [P, T], U32) for a in range(2)]
+        t1w = [sbuf("t1w%d" % a, [P, T], U32) for a in range(2)]
+        w1_raw = {(g, a): sbuf("w1_raw%d%d" % (g, a), [P, 4, G], F32) for g in range(2) for a in range(2)}
+        w4_raw = [sbuf("w4_raw%d" % g, [P, 4, N], F32) for g in range(2)]
+        gain_sb = sbuf("gain_sb", [P, 2, 16], F32)
+
+        def load_words(dst, words):
+            nc.sync.dma_start(out=dst[:].bitcast(I32), in_=words.rearrange("p t i -> p (t i)").bitcast(I32))
+
+        def load_w1(g, a):
+            nc.sync.dma_start(out=w1_raw[g, a][:], in_=w1[G * a : G * (a + 1), G * g : G * (g + 1)].rearrange("(p j) c -> p j c", j=4))
+
+        def load_plane(eng, dst, scales):
+            for q in range(4):
+                eng.dma_start(out=dst[32 * q : 32 * q + 4, :].bitcast(I32), in_=scales[0, 4 * q : 4 * q + 4, :].bitcast(I32))
+
+        def load_two_planes(eng, dst, scales):
+            for q in range(4):
+                eng.dma_start(
+                    out=dst[32 * q : 32 * q + 4, :, :].bitcast(I32),
+                    in_=scales[:, 4 * q : 4 * q + 4, :].rearrange("a r t -> r a t").bitcast(I32),
+                )
+
+        def load_tab_planes(eng):
+            for q in range(4):
+                eng.dma_start(
+                    out=t1s[32 * q + TAB_ROW : 32 * q + TAB_ROW + 8, :].bitcast(I32),
+                    in_=tab_scales[:, 4 * q : 4 * q + 4, :].bitcast(I32),
+                )
+
+        def load_gain(eng):
+            gain_runs = gain.rearrange("(g u c) -> u g c", g=2, c=16)
+            for i in range(4):
+                eng.dma_start(out=gain_sb[i:P:4, :, 0:13], in_=gain_runs[:, :, i : i + 13])
+
+        nc.sync.dma_start(idx3[:], offs3)
+        nc.sync.dma_start(out=t3w[:].bitcast(I32), in_=tab3_words[0].bitcast(I32))
+        load_words(w3w_raw, w3_words[0])
+        nc.sync.dma_start(idx2[:], offs2)
+        load_plane(nc.sync, t3s, tab3_scales)
+        load_words(t2w[0], tab2_words[0])
+        load_plane(nc.sync, w3s_raw, w3_scales)
+        nc.sync.dma_start(out=w2w_raw[:], in_=w2_words.rearrange("a p c -> p a c").bitcast(I32))
+        load_two_planes(nc.sync, t2s, tab2_scales)
+        nc.sync.dma_start(idx[:], offs)
+        load_words(t2w[1], tab2_words[1])
+        load_two_planes(nc.sync, w2s_raw, w2_scales)
+        load_w1(0, 0)
+        load_tab_planes(nc.sync)
+        load_words(t1w[0], tab_words[0])
+        load_gain(nc.sync)
+        load_w1(0, 1)
+        load_words(t1w[1], tab_words[1])
+        load_w1(1, 0)
+        load_w1(1, 1)
+        for g in range(2):
+            rows = w4[G * g : G * (g + 1), :].rearrange("(u t i) n -> t u i n", t=4, i=4)
+            for t in range(4):
+                nc.sync.dma_start(out=w4_raw[g][:, t, :], in_=rows[t])
+
+        def gather(name, window, offsets, dtype):
+            picked = sbuf(name, [P, S], dtype)
+            nc.vector.tensor_copy(picked[:], window.indirect(offsets[:]))
+            return picked
+
+        def quantise(name, src):
+            codes = sbuf(name + "_codes", [P, G], U32)
+            scales = sbuf(name + "_scales", [P, G], U8)
+            nc.vector.quantize_mx(out=codes[:].bitcast(FP8X4), scales=scales[:], in_=src[:])
+            return codes, scales
+
+        def deal_scales(name, raw, groups):
+            dealt = sbuf(name, [P, groups * G], U8)
+            nc.vector.tensor_copy(
+                out=dealt[:].bitcast(I32).rearrange("p (g t u) -> p g u t", t=4, u=32),
+                in_=raw.bitcast(I32).rearrange("p (g u t) -> p g u t", t=4, u=32),
+            )
+            return dealt
+
+        def copy_on(engine, out, in_):
+            if engine == "vector":
+                nc.vector.tensor_copy(out=out, in_=in_)
+            else:
+                nc.scalar.copy(out=out, in_=in_)
+
+        def prepare_w1(g, a, engines):
+            rounded = sbuf("w1_bf%d%d" % (g, a), [P, 4 * G], BF16, "w1_bf%d" % a)
+            dst = rounded[:].rearrange("p (t u i j) -> p t u j i", t=4, i=4, j=4)
+            src = w1_raw[g, a][:].rearrange("p j (u t i) -> p t u j i", t=4, i=4)
+            for half, engine in enumerate(engines):
+                copy_on(engine, dst[:, 2 * half : 2 * half + 2], src[:, 2 * half : 2 * half + 2])
+            return rounded
+
+        def prepare_w4(g, engines):
+            rounded = sbuf("w4_bf%d" % g, [P, 4 * N], BF16)
+            dst = rounded[:].rearrange("p (t m j) -> p m j t", t=4, j=4)
+            src = w4_raw[g][:].rearrange("p j (m t) -> p m j t", t=4)
+            for half, engine in enumerate(engines):
+                copy_on(engine, dst[:, 64 * half : 64 * half + 64], src[:, 64 * half : 64 * half + 64])
+            return rounded
+
+        def interleave(name, planes, shares, tag=""):
+            woven = sbuf(name, [P, 4 * S], BF16, tag)
+            dst = woven[:].rearrange("p (c i t) -> p c t i", i=4, t=4)
+            src = planes[:].rearrange("p t (c i) -> p c t i", i=4)
+            for lo, hi, engine in shares:
+                copy_on(engine, dst[:, lo:hi], src[:, lo:hi])
+            return woven
+
+        v3w = gather("v3w", t3w[:], idx3, U16)
+        w3w = sbuf("w3w", [P, H], I32)
+        nc.vector.tensor_copy(
+            out=w3w[:].rearrange("p (g t u i) -> p g t u i", t=4, u=32, i=4),
+            in_=w3w_raw[:].rearrange("p (g u t i) -> p g t u i", t=4, u=32, i=4),
+        )
+        v3s = gather("v3s", t3s[:], idx3, U8)
+        w3s = deal_scales("w3s", w3s_raw[:], 2)
+        v2w = [gather("v2w0", t2w[0][:], idx2, U32)]
+
+        def field_pass(acc, g, t, start, stop):
+            cols = slice(G * g + P * t, G * g + P * (t + 1))
+            nc.tensor.matmul_mx(out=acc[:], lhsT=w3w[:, cols].bitcast(FP8X4), lhsT_scale=w3s[:, cols],
+                                rhs=v3w[:].bitcast(FP4X4), rhs_scale=v3s[:], start=start, stop=stop)
+
+        field = []
+        for t in range(4):
+            acc = bank("low%d" % t, "field%d" % t)
+            field_pass(acc, 0, t, True, True)
+            kept = sbuf("field_sb%d" % t, [P, S], F32)
+            nc.scalar.copy(out=kept[:], in_=acc[:])
+            field.append(kept)
+
+        v2s = [gather("v2s%d" % a, t2s[:, a, :], idx2, U8) for a in range(2)]
+        w2w = sbuf("w2w", [P, H], I32)
+        nc.vector.tensor_copy(
+            out=w2w[:].rearrange("p (b t u e) -> p b u t e", t=4, u=32, e=2),
+            in_=w2w_raw[:].rearrange("p a c -> p (a c)").rearrange("p (b u t e) -> p b u t e", t=4, u=32, e=2),
+        )
+        w2s = deal_scales("w2s", w2s_raw[:].rearrange("p a c -> p (a c)"), 4)
+        v2w.append(gather("v2w1", t2w[1][:], idx2, U32))
+
+        def opp_pass(acc, g, t, a, start, stop):
+            c0 = H * a + G * g + P * t
+            nc.tensor.matmul_mx(out=acc[:], lhsT=w2w[:, c0 // 2 : (c0 + P) // 2].bitcast(FP4X4), lhsT_scale=w2s[:, c0 : c0 + P],
+                                rhs=v2w[a][:].bitcast(FP8X4), rhs_scale=v2s[a][:], start=start, stop=stop)
+
+        def gain_of(g, t):
+            return gain_sb[:, g, 4 * t : 4 * t + 1]
+
+        opp_hi = [bank("high%d" % t, "opp_hi%d" % t) for t in range(4)]
+        opp_lo = [bank("low%d" % t, "opp_lo%d" % t) for t in range(4)]
+        for t in range(4):
+            field_pass(opp_hi[t], 1, t, True, False)
+        for t in range(4):
+            opp_pass(opp_lo[t], 0, t, 0, True, False)
+            opp_pass(opp_lo[t], 0, t, 1, False, True)
+        for t in range(4):
+            opp_pass(opp_hi[t], 1, t, 0, False, False)
+            opp_pass(opp_hi[t], 1, t, 1, False, True)
+
+        x2 = sbuf("x2", [P, 4, S], F32, "x")
+        for t in range(4):
+            nc.vector.tensor_tensor(out=x2[:, t, :], in0=opp_lo[t][:], in1=field[t][:], op=ADD)
+        w1_bf = {(0, 0): prepare_w1(0, 0, ("scalar", "scalar"))}
+        e2 = [sbuf("e2_lo", [P, 4, S], F32, "w1_raw00"), sbuf("e2_hi", [P, 4, S], F32)]
+        for t in range(4):
+            nc.scalar.activation(out=e2[0][:, t, :], in_=x2[:, t, :], func=GELU)
+        for t in range(4):
+            nc.scalar.activation(out=e2[1][:, t, :], in_=opp_hi[t][:], func=GELU)
+
+        team_hi = [bank("high%d" % t, "team_hi%d" % t) for t in range(4)]
+        v1s = gather("v1s", t1s[:], idx, U8)
+        v1w = [gather("v1w0", t1w[0][:], idx, U32)]
+        w1q = {(0, 0): quantise("w1q00", w1_bf[0, 0])}
+
+        def team_pass(acc, g, t, a, start, stop):
+            codes, scales = w1q[g, a]
+            cols = slice(P * t, P * (t + 1))
+            nc.tensor.matmul_mx(out=acc[:], lhsT=codes[:, cols].bitcast(FP8X4), lhsT_scale=scales[:, cols],
+                                rhs=v1w[a][:].bitcast(FP8X4), rhs_scale=v1s[TAB_ROW + 4 * a : P, :], start=start, stop=stop)
+
+        team_lo = [bank("low%d" % t, "team_lo%d" % t) for t in range(4)]
+        for t in range(4):
+            team_pass(team_lo[t], 0, t, 0, True, False)
+        for t in range(4):
+            field_pass(team_hi[t], 1, t, True, False)
+
+        for t in range(4):
+            nc.vector.tensor_scalar(out=e2[0][:, t, :], in0=e2[0][:, t, :], scalar1=gain_of(0, t), scalar2=None, op0=MULT)
+        w1_bf[0, 1] = prepare_w1(0, 1, ("vector", "vector"))
+        w1q[0, 1] = quantise("w1q01", w1_bf[0, 1])
+        for t in range(4):
+            nc.scalar.activation(out=e2[1][:, t, :], in_=e2[1][:, t, :], func=COPY, scale=gain_of(1, t))
+        v1w.append(gather("v1w1", t1w[1][:], idx, U32))
+        for t in range(4):
+            team_pass(team_lo[t], 0, t, 1, False, True)
+
+        def difference(g, e1):
+            planes = sbuf("h_planes%d" % g, [P, 4, S], BF16)
+            for t in range(4):
+                nc.vector.scalar_tensor_tensor(out=planes[:, t, :], in0=e1[:, t, :], scalar=gain_of(g, t), in1=e2[g][:, t, :], op0=MULT, op1=SUBTRACT)
+            return planes
+
+        x1 = sbuf("x1", [P, 4, S], F32, "x")
+        for t in range(4):
+            nc.vector.tensor_tensor(out=x1[:, t, :], in0=team_lo[t][:], in1=field[t][:], op=ADD)
+        w1_bf[1, 0] = prepare_w1(1, 0, ("scalar", "scalar"))
+        w1q[1, 0] = quantise("w1q10", w1_bf[1, 0])
+        for t in range(4):
+            team_pass(team_hi[t], 1, t, 0, False, False)
+        e1_lo = sbuf("e1_lo", [P, 4, S], F32, "w1_raw10")
+        for t in range(4):
+            nc.scalar.activation(out=e1_lo[:, t, :], in_=x1[:, t, :], func=GELU)
+        w1_bf[1, 1] = prepare_w1(1, 1, ("vector", "vector"))
+        w1q[1, 1] = quantise("w1q11", w1_bf[1, 1])
+        for t in range(4):
+            team_pass(team_hi[t], 1, t, 1, False, True)
+        planes_lo = difference(0, e1_lo)
+        w4_bf0 = prepare_w4(0, ("scalar", "vector"))
+        e1_hi = sbuf("e1_hi", [P, 4, S], F32, "w1_raw01")
+        for t in range(4):
+            nc.scalar.activation(out=e1_hi[:, t, :], in_=team_hi[t][:], func=GELU)
+        planes_hi = difference(1, e1_hi)
+        w4_bf1 = prepare_w4(1, ("scalar", "scalar"))
+        h_lo = interleave("h_bf0", planes_lo, ((0, 128, "vector"),), "w1_raw01")
+        w4q = [quantise("w4q0", w4_bf0)]
+        hq = [quantise("hq0", h_lo)]
+
+        def out_pass(acc, t, g):
+            cols = slice(P * t, P * (t + 1))
+            nc.tensor.matmul_mx(out=acc[:], lhsT=w4q[g][0][:, cols].bitcast(FP8X4), lhsT_scale=w4q[g][1][:, cols],
+                                rhs=hq[g][0][:].bitcast(FP8X4), rhs_scale=hq[g][1][:], start=(g == 0), stop=(g == 1))
+
+        y_acc = [bank("low%d" % t, "y%d" % t) for t in range(4)]
+        for t in range(4):
+            out_pass(y_acc[t], t, 0)
+        h_hi = interleave("h_bf1", planes_hi, ((0, 32, "vector"), (32, 128, "scalar")))
+        w4q.append(quantise("w4q1", w4_bf1))
+        hq.append(quantise("hq1", h_hi))
+        y = sbuf("y_sb", [P, 4, S], F32)
+        y_rows = out_0.rearrange("(p t) s -> p t s", t=4)
+        for t in range(4):
+            out_pass(y_acc[t], t, 1)
+            copy_on("scalar" if t % 2 == 0 else "vector", y[:, t, :], y_acc[t][:])
+            nc.sync.dma_start(out=y_rows[:, t, :], in_=y[:, t, :])
+        y_codes, y_scales = quantise("yq", interleave("y_bf", y, ((0, 80, "vector"), (80, 128, "scalar"))))
+        nc.sync.dma_start(out=out_1[0].rearrange("p m t -> p (m t)").bitcast(I32), in_=y_codes[:].bitcast(I32))
+        for q in range(4):
+            nc.sync.dma_start(out=out_2[0, 4 * q : 4 * q + 4, :].bitcast(I32), in_=y_scales[32 * q : 32 * q + 4, :].bitcast(I32))

@@ -21,7 +21,7 @@ SUBTRACT = mybir.AluOpType.subtract
 
 P = 128
 G = 512
-TAB_ROW = 8
+TAB_ROW = 4
 
 
 def tile_list_lacrosse_matchup_features_kernel(
@@ -47,11 +47,13 @@ def tile_list_lacrosse_matchup_features_kernel(
         t3s = sbuf("t3s", [P, T3], U8)
         w3s_raw = sbuf("w3s_raw", [P, H], U8)
         w2s_raw = sbuf("w2s_raw", [P, 2, H], U8)
-        t2s = sbuf("t2s", [P, 2, T], U8)
+        t2s = sbuf("t2s", [P, T], U8)
+        v2s = sbuf("v2s", [P, 2, S], U8)
+        v1s = sbuf("v1s", [P, 2, S], U8)
         t1s = sbuf("t1s", [P, T], U8)
-        for plane in (t3s[:], w3s_raw[:], w2s_raw[:].rearrange("p a c -> p (a c)")):
+        for plane in (t1s[:], w3s_raw[:], v2s[:].rearrange("p a c -> p (a c)"), v1s[:].rearrange("p a c -> p (a c)")):
             nc.gpsimd.memset(plane.bitcast(I32), 0)
-        for plane in (t2s[:].rearrange("p a c -> p (a c)"), t1s[:]):
+        for plane in (t2s[:], t3s[:], w2s_raw[:].rearrange("p a c -> p (a c)")):
             nc.vector.memset(plane.bitcast(I32), 0)
 
         t3w = sbuf("t3w", [P, T3], U16)
@@ -70,42 +72,35 @@ def tile_list_lacrosse_matchup_features_kernel(
             nc.sync.dma_start(out=w1_raw[g, a][:], in_=w1[G * a : G * (a + 1), G * g : G * (g + 1)].rearrange("(p j) c -> p j c", j=4))
 
         def load_plane(eng, dst, scales):
-            for q in range(4):
-                eng.dma_start(out=dst[32 * q : 32 * q + 4, :].bitcast(I32), in_=scales[0, 4 * q : 4 * q + 4, :].bitcast(I32))
+            for r in range(4):
+                eng.dma_start(out=dst[r:P:32, :].bitcast(I32), in_=scales[0, r:16:4, :].bitcast(I32))
+
+        def load_spread(dst, scales):
+            nc.sync.dma_start(out=dst[0:P:4, :].bitcast(I32), in_=scales.rearrange("a q t -> q a t").bitcast(I32))
 
         def load_two_planes(eng, dst, scales):
-            for q in range(4):
-                eng.dma_start(
-                    out=dst[32 * q : 32 * q + 4, :, :].bitcast(I32),
-                    in_=scales[:, 4 * q : 4 * q + 4, :].rearrange("a r t -> r a t").bitcast(I32),
-                )
-
-        def load_tab_planes(eng):
-            for q in range(4):
-                eng.dma_start(
-                    out=t1s[32 * q + TAB_ROW : 32 * q + TAB_ROW + 8, :].bitcast(I32),
-                    in_=tab_scales[:, 4 * q : 4 * q + 4, :].bitcast(I32),
-                )
+            for r in range(4):
+                eng.dma_start(out=dst[r:P:32, :, :].bitcast(I32), in_=scales[:, r:16:4, :].rearrange("a q t -> q a t").bitcast(I32))
 
         def load_gain(eng):
             gain_runs = gain.rearrange("(g u c) -> u g c", g=2, c=16)
             for i in range(4):
                 eng.dma_start(out=gain_sb[i:P:4, :, 0:13], in_=gain_runs[:, :, i : i + 13])
 
+        nc.sync.dma_start(idx2[:], offs2)
+        load_spread(t2s, tab2_scales)
         nc.sync.dma_start(idx3[:], offs3)
         nc.sync.dma_start(out=t3w[:].bitcast(I32), in_=tab3_words[0].bitcast(I32))
         load_words(w3w_raw, w3_words[0])
-        nc.sync.dma_start(idx2[:], offs2)
         load_plane(nc.sync, t3s, tab3_scales)
         load_words(t2w[0], tab2_words[0])
         load_plane(nc.sync, w3s_raw, w3_scales)
         nc.sync.dma_start(out=w2w_raw[:], in_=w2_words.rearrange("a p c -> p a c").bitcast(I32))
-        load_two_planes(nc.sync, t2s, tab2_scales)
         nc.sync.dma_start(idx[:], offs)
-        load_words(t2w[1], tab2_words[1])
+        load_spread(t1s, tab_scales)
         load_two_planes(nc.sync, w2s_raw, w2_scales)
+        load_words(t2w[1], tab2_words[1])
         load_w1(0, 0)
-        load_tab_planes(nc.sync)
         load_words(t1w[0], tab_words[0])
         load_gain(nc.sync)
         load_w1(0, 1)
@@ -117,8 +112,8 @@ def tile_list_lacrosse_matchup_features_kernel(
             for t in range(4):
                 nc.sync.dma_start(out=w4_raw[g][:, t, :], in_=rows[t])
 
-        def gather(name, window, offsets, dtype):
-            picked = sbuf(name, [P, S], dtype)
+        def gather(name, window, offsets, dtype, tag=""):
+            picked = sbuf(name, [P, S], dtype, tag)
             nc.vector.tensor_copy(picked[:], window.indirect(offsets[:]))
             return picked
 
@@ -143,7 +138,7 @@ def tile_list_lacrosse_matchup_features_kernel(
                 nc.scalar.copy(out=out, in_=in_)
 
         def prepare_w1(g, a, engines):
-            rounded = sbuf("w1_bf%d%d" % (g, a), [P, 4 * G], BF16, "w1_bf%d" % a)
+            rounded = sbuf("w1_bf%d%d" % (g, a), [P, 4 * G], BF16, "w1_bf%d" % (2 * g + a))
             dst = rounded[:].rearrange("p (t u i j) -> p t u j i", t=4, i=4, j=4)
             src = w1_raw[g, a][:].rearrange("p j (u t i) -> p t u j i", t=4, i=4)
             for half, engine in enumerate(engines):
@@ -166,6 +161,11 @@ def tile_list_lacrosse_matchup_features_kernel(
                 copy_on(engine, dst[:, lo:hi], src[:, lo:hi])
             return woven
 
+        def place_scales(planes, row, picked):
+            for q in range(4):
+                nc.gpsimd.dma_start(out=planes[32 * q + row : 32 * q + row + 4, :, :].bitcast(I32), in_=picked[32 * q : 32 * q + 32 : 4, :].bitcast(I32))
+
+        place_scales(v2s, 0, gather("v2s_rows", t2s[:], idx2, U8))
         v3w = gather("v3w", t3w[:], idx3, U16)
         w3w = sbuf("w3w", [P, H], I32)
         nc.vector.tensor_copy(
@@ -189,7 +189,7 @@ def tile_list_lacrosse_matchup_features_kernel(
             nc.scalar.copy(out=kept[:], in_=acc[:])
             field.append(kept)
 
-        v2s = [gather("v2s%d" % a, t2s[:, a, :], idx2, U8) for a in range(2)]
+        place_scales(v1s, TAB_ROW, gather("v1s_rows", t1s[:], idx, U8))
         w2w = sbuf("w2w", [P, H], I32)
         nc.vector.tensor_copy(
             out=w2w[:].rearrange("p (b t u e) -> p b u t e", t=4, u=32, e=2),
@@ -201,7 +201,7 @@ def tile_list_lacrosse_matchup_features_kernel(
         def opp_pass(acc, g, t, a, start, stop):
             c0 = H * a + G * g + P * t
             nc.tensor.matmul_mx(out=acc[:], lhsT=w2w[:, c0 // 2 : (c0 + P) // 2].bitcast(FP4X4), lhsT_scale=w2s[:, c0 : c0 + P],
-                                rhs=v2w[a][:].bitcast(FP8X4), rhs_scale=v2s[a][:], start=start, stop=stop)
+                                rhs=v2w[a][:].bitcast(FP8X4), rhs_scale=v2s[:, a, :], start=start, stop=stop)
 
         def gain_of(g, t):
             return gain_sb[:, g, 4 * t : 4 * t + 1]
@@ -214,29 +214,28 @@ def tile_list_lacrosse_matchup_features_kernel(
             opp_pass(opp_lo[t], 0, t, 0, True, False)
             opp_pass(opp_lo[t], 0, t, 1, False, True)
         for t in range(4):
-            opp_pass(opp_hi[t], 1, t, 0, False, False)
-            opp_pass(opp_hi[t], 1, t, 1, False, True)
+            opp_pass(opp_hi[t], 1, t, 1, False, False)
+            opp_pass(opp_hi[t], 1, t, 0, False, True)
 
+        w1_bf = {(0, 0): prepare_w1(0, 0, ("scalar", "scalar"))}
         x2 = sbuf("x2", [P, 4, S], F32, "x")
         for t in range(4):
             nc.vector.tensor_tensor(out=x2[:, t, :], in0=opp_lo[t][:], in1=field[t][:], op=ADD)
-        w1_bf = {(0, 0): prepare_w1(0, 0, ("scalar", "scalar"))}
-        e2 = [sbuf("e2_lo", [P, 4, S], F32, "w1_raw00"), sbuf("e2_hi", [P, 4, S], F32)]
+        e2 = [sbuf("e2_lo", [P, 4, S], F32, "w1_raw00"), sbuf("e2_hi", [P, 4, S], F32, "w1_bf0")]
         for t in range(4):
             nc.scalar.activation(out=e2[0][:, t, :], in_=x2[:, t, :], func=GELU)
+        w1q = {(0, 0): quantise("w1q00", w1_bf[0, 0])}
         for t in range(4):
             nc.scalar.activation(out=e2[1][:, t, :], in_=opp_hi[t][:], func=GELU)
 
         team_hi = [bank("high%d" % t, "team_hi%d" % t) for t in range(4)]
-        v1s = gather("v1s", t1s[:], idx, U8)
         v1w = [gather("v1w0", t1w[0][:], idx, U32)]
-        w1q = {(0, 0): quantise("w1q00", w1_bf[0, 0])}
 
         def team_pass(acc, g, t, a, start, stop):
             codes, scales = w1q[g, a]
             cols = slice(P * t, P * (t + 1))
             nc.tensor.matmul_mx(out=acc[:], lhsT=codes[:, cols].bitcast(FP8X4), lhsT_scale=scales[:, cols],
-                                rhs=v1w[a][:].bitcast(FP8X4), rhs_scale=v1s[TAB_ROW + 4 * a : P, :], start=start, stop=stop)
+                                rhs=v1w[a][:].bitcast(FP8X4), rhs_scale=v1s[TAB_ROW:P, a, :], start=start, stop=stop)
 
         team_lo = [bank("low%d" % t, "team_lo%d" % t) for t in range(4)]
         for t in range(4):
@@ -244,20 +243,22 @@ def tile_list_lacrosse_matchup_features_kernel(
         for t in range(4):
             field_pass(team_hi[t], 1, t, True, False)
 
-        for t in range(4):
-            nc.vector.tensor_scalar(out=e2[0][:, t, :], in0=e2[0][:, t, :], scalar1=gain_of(0, t), scalar2=None, op0=MULT)
         w1_bf[0, 1] = prepare_w1(0, 1, ("vector", "vector"))
         w1q[0, 1] = quantise("w1q01", w1_bf[0, 1])
+        e2g = [e2[0]]
         for t in range(4):
-            nc.scalar.activation(out=e2[1][:, t, :], in_=e2[1][:, t, :], func=COPY, scale=gain_of(1, t))
+            nc.scalar.activation(out=e2g[0][:, t, :], in_=e2[0][:, t, :], func=COPY, scale=gain_of(0, t))
         v1w.append(gather("v1w1", t1w[1][:], idx, U32))
+        e2g.append(sbuf("e2g_hi", [P, 4, S], F32, "t1w1"))
+        for t in range(4):
+            nc.vector.tensor_scalar(out=e2g[1][:, t, :], in0=e2[1][:, t, :], scalar1=gain_of(1, t), scalar2=None, op0=MULT)
         for t in range(4):
             team_pass(team_lo[t], 0, t, 1, False, True)
 
         def difference(g, e1):
             planes = sbuf("h_planes%d" % g, [P, 4, S], BF16)
             for t in range(4):
-                nc.vector.scalar_tensor_tensor(out=planes[:, t, :], in0=e1[:, t, :], scalar=gain_of(g, t), in1=e2[g][:, t, :], op0=MULT, op1=SUBTRACT)
+                nc.vector.scalar_tensor_tensor(out=planes[:, t, :], in0=e1[:, t, :], scalar=gain_of(g, t), in1=e2g[g][:, t, :], op0=MULT, op1=SUBTRACT)
             return planes
 
         x1 = sbuf("x1", [P, 4, S], F32, "x")
@@ -275,15 +276,8 @@ def tile_list_lacrosse_matchup_features_kernel(
         for t in range(4):
             team_pass(team_hi[t], 1, t, 1, False, True)
         planes_lo = difference(0, e1_lo)
-        w4_bf0 = prepare_w4(0, ("scalar", "vector"))
-        e1_hi = sbuf("e1_hi", [P, 4, S], F32, "w1_raw01")
-        for t in range(4):
-            nc.scalar.activation(out=e1_hi[:, t, :], in_=team_hi[t][:], func=GELU)
-        planes_hi = difference(1, e1_hi)
-        w4_bf1 = prepare_w4(1, ("scalar", "scalar"))
-        h_lo = interleave("h_bf0", planes_lo, ((0, 128, "vector"),), "w1_raw01")
-        w4q = [quantise("w4q0", w4_bf0)]
-        hq = [quantise("hq0", h_lo)]
+        hq = [quantise("hq0", interleave("h_bf0", planes_lo, ((0, 128, "vector"),)))]
+        w4q = [quantise("w4q0", prepare_w4(0, ("scalar", "scalar")))]
 
         def out_pass(acc, t, g):
             cols = slice(P * t, P * (t + 1))
@@ -293,7 +287,12 @@ def tile_list_lacrosse_matchup_features_kernel(
         y_acc = [bank("low%d" % t, "y%d" % t) for t in range(4)]
         for t in range(4):
             out_pass(y_acc[t], t, 0)
-        h_hi = interleave("h_bf1", planes_hi, ((0, 32, "vector"), (32, 128, "scalar")))
+        e1_hi = sbuf("e1_hi", [P, 4, S], F32, "w1_raw01")
+        for t in range(4):
+            nc.scalar.activation(out=e1_hi[:, t, :], in_=team_hi[t][:], func=GELU)
+        planes_hi = difference(1, e1_hi)
+        w4_bf1 = prepare_w4(1, ("scalar", "scalar"))
+        h_hi = interleave("h_bf1", planes_hi, ((0, 80, "vector"), (80, 128, "scalar")))
         w4q.append(quantise("w4q1", w4_bf1))
         hq.append(quantise("hq1", h_hi))
         y = sbuf("y_sb", [P, 4, S], F32)
@@ -304,5 +303,6 @@ def tile_list_lacrosse_matchup_features_kernel(
             nc.sync.dma_start(out=y_rows[:, t, :], in_=y[:, t, :])
         y_codes, y_scales = quantise("yq", interleave("y_bf", y, ((0, 80, "vector"), (80, 128, "scalar"))))
         nc.sync.dma_start(out=out_1[0].rearrange("p m t -> p (m t)").bitcast(I32), in_=y_codes[:].bitcast(I32))
-        for q in range(4):
-            nc.sync.dma_start(out=out_2[0, 4 * q : 4 * q + 4, :].bitcast(I32), in_=y_scales[32 * q : 32 * q + 4, :].bitcast(I32))
+        for r in range(4):
+            queue = nc.scalar if r % 2 == 0 else nc.sync
+            queue.dma_start(out=out_2[0, r:16:4, :].bitcast(I32), in_=y_scales[r:P:32, :].bitcast(I32))

@@ -21,7 +21,7 @@ SUBTRACT = mybir.AluOpType.subtract
 
 P = 128
 G = 512
-TAB_ROW = 4
+TAB_ROW = 8
 
 
 def tile_list_lacrosse_matchup_features_kernel(
@@ -47,13 +47,11 @@ def tile_list_lacrosse_matchup_features_kernel(
         t3s = sbuf("t3s", [P, T3], U8)
         w3s_raw = sbuf("w3s_raw", [P, H], U8)
         w2s_raw = sbuf("w2s_raw", [P, 2, H], U8)
-        t2s = sbuf("t2s", [P, T], U8)
-        v2s = sbuf("v2s", [P, 2, S], U8)
-        v1s = sbuf("v1s", [P, 2, S], U8)
+        t2s = sbuf("t2s", [P, 2, T], U8)
         t1s = sbuf("t1s", [P, T], U8)
-        for plane in (t1s[:], w3s_raw[:], v2s[:].rearrange("p a c -> p (a c)"), v1s[:].rearrange("p a c -> p (a c)")):
+        for plane in (t3s[:], w3s_raw[:], w2s_raw[:].rearrange("p a c -> p (a c)")):
             nc.gpsimd.memset(plane.bitcast(I32), 0)
-        for plane in (t2s[:], t3s[:], w2s_raw[:].rearrange("p a c -> p (a c)")):
+        for plane in (t2s[:].rearrange("p a c -> p (a c)"), t1s[:]):
             nc.vector.memset(plane.bitcast(I32), 0)
 
         t3w = sbuf("t3w", [P, T3], U16)
@@ -75,8 +73,12 @@ def tile_list_lacrosse_matchup_features_kernel(
             for r in range(4):
                 eng.dma_start(out=dst[r:P:32, :].bitcast(I32), in_=scales[0, r:16:4, :].bitcast(I32))
 
-        def load_spread(dst, scales):
-            nc.sync.dma_start(out=dst[0:P:4, :].bitcast(I32), in_=scales.rearrange("a q t -> q a t").bitcast(I32))
+        def load_tab_planes(eng):
+            for q in range(4):
+                eng.dma_start(
+                    out=t1s[32 * q + TAB_ROW : 32 * q + TAB_ROW + 8, :].bitcast(I32),
+                    in_=tab_scales[:, 4 * q : 4 * q + 4, :].bitcast(I32),
+                )
 
         def load_two_planes(eng, dst, scales):
             for r in range(4):
@@ -87,20 +89,20 @@ def tile_list_lacrosse_matchup_features_kernel(
             for i in range(4):
                 eng.dma_start(out=gain_sb[i:P:4, :, 0:13], in_=gain_runs[:, :, i : i + 13])
 
-        nc.sync.dma_start(idx2[:], offs2)
-        load_spread(t2s, tab2_scales)
         nc.sync.dma_start(idx3[:], offs3)
         nc.sync.dma_start(out=t3w[:].bitcast(I32), in_=tab3_words[0].bitcast(I32))
         load_words(w3w_raw, w3_words[0])
+        nc.sync.dma_start(idx2[:], offs2)
         load_plane(nc.sync, t3s, tab3_scales)
         load_words(t2w[0], tab2_words[0])
         load_plane(nc.sync, w3s_raw, w3_scales)
         nc.sync.dma_start(out=w2w_raw[:], in_=w2_words.rearrange("a p c -> p a c").bitcast(I32))
+        load_two_planes(nc.sync, t2s, tab2_scales)
         nc.sync.dma_start(idx[:], offs)
-        load_spread(t1s, tab_scales)
-        load_two_planes(nc.sync, w2s_raw, w2_scales)
         load_words(t2w[1], tab2_words[1])
+        load_two_planes(nc.sync, w2s_raw, w2_scales)
         load_w1(0, 0)
+        load_tab_planes(nc.sync)
         load_words(t1w[0], tab_words[0])
         load_gain(nc.sync)
         load_w1(0, 1)
@@ -126,8 +128,8 @@ def tile_list_lacrosse_matchup_features_kernel(
         def deal_scales(name, raw, groups):
             dealt = sbuf(name, [P, groups * G], U8)
             nc.vector.tensor_copy(
-                out=dealt[:].bitcast(I32).rearrange("p (g t u) -> p g u t", t=4, u=32),
-                in_=raw.bitcast(I32).rearrange("p (g u t) -> p g u t", t=4, u=32),
+                out=dealt[:].bitcast(I32).rearrange("p (g t u) -> p g t u", t=4, u=32),
+                in_=raw.bitcast(I32).rearrange("p (g u t) -> p g t u", t=4, u=32),
             )
             return dealt
 
@@ -161,11 +163,6 @@ def tile_list_lacrosse_matchup_features_kernel(
                 copy_on(engine, dst[:, lo:hi], src[:, lo:hi])
             return woven
 
-        def place_scales(planes, row, picked):
-            for q in range(4):
-                nc.gpsimd.dma_start(out=planes[32 * q + row : 32 * q + row + 4, :, :].bitcast(I32), in_=picked[32 * q : 32 * q + 32 : 4, :].bitcast(I32))
-
-        place_scales(v2s, 0, gather("v2s_rows", t2s[:], idx2, U8))
         v3w = gather("v3w", t3w[:], idx3, U16)
         w3w = sbuf("w3w", [P, H], I32)
         nc.vector.tensor_copy(
@@ -189,11 +186,11 @@ def tile_list_lacrosse_matchup_features_kernel(
             nc.scalar.copy(out=kept[:], in_=acc[:])
             field.append(kept)
 
-        place_scales(v1s, TAB_ROW, gather("v1s_rows", t1s[:], idx, U8))
+        v2s = [gather("v2s%d" % a, t2s[:, a, :], idx2, U8) for a in range(2)]
         w2w = sbuf("w2w", [P, H], I32)
         nc.vector.tensor_copy(
-            out=w2w[:].rearrange("p (b t u e) -> p b u t e", t=4, u=32, e=2),
-            in_=w2w_raw[:].rearrange("p a c -> p (a c)").rearrange("p (b u t e) -> p b u t e", t=4, u=32, e=2),
+            out=w2w[:].rearrange("p (b t u e) -> p b t u e", t=4, u=32, e=2),
+            in_=w2w_raw[:].rearrange("p a c -> p (a c)").rearrange("p (b u t e) -> p b t u e", t=4, u=32, e=2),
         )
         w2s = deal_scales("w2s", w2s_raw[:].rearrange("p a c -> p (a c)"), 4)
         v2w.append(gather("v2w1", t2w[1][:], idx2, U32))
@@ -201,7 +198,7 @@ def tile_list_lacrosse_matchup_features_kernel(
         def opp_pass(acc, g, t, a, start, stop):
             c0 = H * a + G * g + P * t
             nc.tensor.matmul_mx(out=acc[:], lhsT=w2w[:, c0 // 2 : (c0 + P) // 2].bitcast(FP4X4), lhsT_scale=w2s[:, c0 : c0 + P],
-                                rhs=v2w[a][:].bitcast(FP8X4), rhs_scale=v2s[:, a, :], start=start, stop=stop)
+                                rhs=v2w[a][:].bitcast(FP8X4), rhs_scale=v2s[a][:], start=start, stop=stop)
 
         def gain_of(g, t):
             return gain_sb[:, g, 4 * t : 4 * t + 1]
@@ -229,13 +226,14 @@ def tile_list_lacrosse_matchup_features_kernel(
             nc.scalar.activation(out=e2[1][:, t, :], in_=opp_hi[t][:], func=GELU)
 
         team_hi = [bank("high%d" % t, "team_hi%d" % t) for t in range(4)]
+        v1s = gather("v1s", t1s[:], idx, U8)
         v1w = [gather("v1w0", t1w[0][:], idx, U32)]
 
         def team_pass(acc, g, t, a, start, stop):
             codes, scales = w1q[g, a]
             cols = slice(P * t, P * (t + 1))
             nc.tensor.matmul_mx(out=acc[:], lhsT=codes[:, cols].bitcast(FP8X4), lhsT_scale=scales[:, cols],
-                                rhs=v1w[a][:].bitcast(FP8X4), rhs_scale=v1s[TAB_ROW:P, a, :], start=start, stop=stop)
+                                rhs=v1w[a][:].bitcast(FP8X4), rhs_scale=v1s[TAB_ROW + 4 * a : P, :], start=start, stop=stop)
 
         team_lo = [bank("low%d" % t, "team_lo%d" % t) for t in range(4)]
         for t in range(4):

@@ -22,6 +22,7 @@ SUBTRACT = mybir.AluOpType.subtract
 P = 128
 G = 512
 TAB_ROW = 8
+REPEATED = (0, 0, 0, 384)
 
 
 def tile_list_lacrosse_matchup_features_kernel(
@@ -119,8 +120,8 @@ def tile_list_lacrosse_matchup_features_kernel(
             nc.vector.tensor_copy(picked[:], window.indirect(offsets[:]))
             return picked
 
-        def quantise(name, src):
-            codes = sbuf(name + "_codes", [P, G], U32)
+        def quantise(name, src, tag=""):
+            codes = sbuf(name + "_codes", [P, G], U32, tag)
             scales = sbuf(name + "_scales", [P, G], U8)
             nc.vector.quantize_mx(out=codes[:].bitcast(FP8X4), scales=scales[:], in_=src[:])
             return codes, scales
@@ -143,16 +144,16 @@ def tile_list_lacrosse_matchup_features_kernel(
             rounded = sbuf("w1_bf%d%d" % (g, a), [P, 4 * G], BF16, "w1_bf%d" % (2 * g + a))
             dst = rounded[:].rearrange("p (t u i j) -> p t u j i", t=4, i=4, j=4)
             src = w1_raw[g, a][:].rearrange("p j (u t i) -> p t u j i", t=4, i=4)
-            for half, engine in enumerate(engines):
-                copy_on(engine, dst[:, 2 * half : 2 * half + 2], src[:, 2 * half : 2 * half + 2])
+            for lo, hi, engine in engines:
+                copy_on(engine, dst[:, lo:hi], src[:, lo:hi])
             return rounded
 
         def prepare_w4(g, engines):
             rounded = sbuf("w4_bf%d" % g, [P, 4 * N], BF16)
             dst = rounded[:].rearrange("p (t m j) -> p m j t", t=4, j=4)
             src = w4_raw[g][:].rearrange("p j (m t) -> p m j t", t=4)
-            for half, engine in enumerate(engines):
-                copy_on(engine, dst[:, 64 * half : 64 * half + 64], src[:, 64 * half : 64 * half + 64])
+            for lo, hi, engine in engines:
+                copy_on(engine, dst[:, lo:hi], src[:, lo:hi])
             return rounded
 
         def interleave(name, planes, shares, tag=""):
@@ -173,18 +174,30 @@ def tile_list_lacrosse_matchup_features_kernel(
         w3s = deal_scales("w3s", w3s_raw[:], 2)
         v2w = [gather("v2w0", t2w[0][:], idx2, U32)]
 
-        def field_pass(acc, g, t, start, stop):
+        def field_pass(acc, g, t, lo, hi, start, stop):
             cols = slice(G * g + P * t, G * g + P * (t + 1))
-            nc.tensor.matmul_mx(out=acc[:], lhsT=w3w[:, cols].bitcast(FP8X4), lhsT_scale=w3s[:, cols],
-                                rhs=v3w[:].bitcast(FP4X4), rhs_scale=v3s[:], start=start, stop=stop)
+            nc.tensor.matmul_mx(out=acc[:, lo:hi], lhsT=w3w[:, cols].bitcast(FP8X4), lhsT_scale=w3s[:, cols],
+                                rhs=v3w[:, lo:hi].bitcast(FP4X4), rhs_scale=v3s[:, lo:hi], start=start, stop=stop)
 
-        field = []
+        def repeat_field(acc, t):
+            for lo in range(0, REPEATED[t], P):
+                field_pass(acc, 0, t, lo, lo + P, False, False)
+
+        field = sbuf("field_sb", [P, 4, S], F32)
         for t in range(4):
             acc = bank("low%d" % t, "field%d" % t)
-            field_pass(acc, 0, t, True, True)
-            kept = sbuf("field_sb%d" % t, [P, S], F32)
-            nc.scalar.copy(out=kept[:], in_=acc[:])
-            field.append(kept)
+            field_pass(acc, 0, t, REPEATED[t], S, True, True)
+            nc.scalar.copy(out=field[:, t, REPEATED[t] : S], in_=acc[:, REPEATED[t] : S])
+
+        def add_field(x, acc):
+            for t in range(4):
+                nc.vector.tensor_tensor(out=x[:, t, REPEATED[t] : S], in0=acc[t][:, REPEATED[t] : S], in1=field[:, t, REPEATED[t] : S], op=ADD)
+
+        def gelu_low(e, x, acc):
+            for t in range(4):
+                if REPEATED[t]:
+                    nc.scalar.activation(out=e[:, t, 0 : REPEATED[t]], in_=acc[t][:, 0 : REPEATED[t]], func=GELU)
+                nc.scalar.activation(out=e[:, t, REPEATED[t] : S], in_=x[:, t, REPEATED[t] : S], func=GELU)
 
         v2s = [gather("v2s%d" % a, t2s[:, a, :], idx2, U8) for a in range(2)]
         w2w = sbuf("w2w", [P, H], I32)
@@ -206,21 +219,20 @@ def tile_list_lacrosse_matchup_features_kernel(
         opp_hi = [bank("high%d" % t, "opp_hi%d" % t) for t in range(4)]
         opp_lo = [bank("low%d" % t, "opp_lo%d" % t) for t in range(4)]
         for t in range(4):
-            field_pass(opp_hi[t], 1, t, True, False)
+            field_pass(opp_hi[t], 1, t, 0, S, True, False)
         for t in range(4):
             opp_pass(opp_lo[t], 0, t, 0, True, False)
+            repeat_field(opp_lo[t], t)
             opp_pass(opp_lo[t], 0, t, 1, False, True)
         for t in range(4):
             opp_pass(opp_hi[t], 1, t, 1, False, False)
             opp_pass(opp_hi[t], 1, t, 0, False, True)
 
-        w1_bf = {(0, 0): prepare_w1(0, 0, ("scalar", "scalar"))}
+        w1_bf = {(0, 0): prepare_w1(0, 0, ((0, 4, "scalar"),))}
         x2 = sbuf("x2", [P, 4, S], F32, "x")
-        for t in range(4):
-            nc.vector.tensor_tensor(out=x2[:, t, :], in0=opp_lo[t][:], in1=field[t][:], op=ADD)
+        add_field(x2, opp_lo)
         e2 = [sbuf("e2_lo", [P, 4, S], F32, "w1_raw00"), sbuf("e2_hi", [P, 4, S], F32, "w1_bf0")]
-        for t in range(4):
-            nc.scalar.activation(out=e2[0][:, t, :], in_=x2[:, t, :], func=GELU)
+        gelu_low(e2[0], x2, opp_lo)
         w1q = {(0, 0): quantise("w1q00", w1_bf[0, 0])}
         for t in range(4):
             nc.scalar.activation(out=e2[1][:, t, :], in_=opp_hi[t][:], func=GELU)
@@ -238,18 +250,20 @@ def tile_list_lacrosse_matchup_features_kernel(
         team_lo = [bank("low%d" % t, "team_lo%d" % t) for t in range(4)]
         for t in range(4):
             team_pass(team_lo[t], 0, t, 0, True, False)
+            repeat_field(team_lo[t], t)
         for t in range(4):
-            field_pass(team_hi[t], 1, t, True, False)
+            field_pass(team_hi[t], 1, t, 0, S, True, False)
 
-        w1_bf[0, 1] = prepare_w1(0, 1, ("vector", "vector"))
+        w1_bf[0, 1] = prepare_w1(0, 1, ((0, 4, "vector"),))
         w1q[0, 1] = quantise("w1q01", w1_bf[0, 1])
         e2g = [e2[0]]
         for t in range(4):
             nc.scalar.activation(out=e2g[0][:, t, :], in_=e2[0][:, t, :], func=COPY, scale=gain_of(0, t))
         v1w.append(gather("v1w1", t1w[1][:], idx, U32))
         e2g.append(sbuf("e2g_hi", [P, 4, S], F32, "t1w1"))
-        for t in range(4):
+        for t in range(2):
             nc.vector.tensor_scalar(out=e2g[1][:, t, :], in0=e2[1][:, t, :], scalar1=gain_of(1, t), scalar2=None, op0=MULT)
+            nc.scalar.activation(out=e2g[1][:, 2 + t, :], in_=e2[1][:, 2 + t, :], func=COPY, scale=gain_of(1, 2 + t))
         for t in range(4):
             team_pass(team_lo[t], 0, t, 1, False, True)
 
@@ -260,37 +274,36 @@ def tile_list_lacrosse_matchup_features_kernel(
             return planes
 
         x1 = sbuf("x1", [P, 4, S], F32, "x")
-        for t in range(4):
-            nc.vector.tensor_tensor(out=x1[:, t, :], in0=team_lo[t][:], in1=field[t][:], op=ADD)
-        w1_bf[1, 0] = prepare_w1(1, 0, ("scalar", "scalar"))
+        add_field(x1, team_lo)
+        w1_bf[1, 0] = prepare_w1(1, 0, ((0, 3, "scalar"), (3, 4, "vector")))
         w1q[1, 0] = quantise("w1q10", w1_bf[1, 0])
         for t in range(4):
             team_pass(team_hi[t], 1, t, 0, False, False)
         e1_lo = sbuf("e1_lo", [P, 4, S], F32, "w1_raw10")
-        for t in range(4):
-            nc.scalar.activation(out=e1_lo[:, t, :], in_=x1[:, t, :], func=GELU)
-        w1_bf[1, 1] = prepare_w1(1, 1, ("vector", "vector"))
+        gelu_low(e1_lo, x1, team_lo)
+        w1_bf[1, 1] = prepare_w1(1, 1, ((0, 4, "vector"),))
         w1q[1, 1] = quantise("w1q11", w1_bf[1, 1])
         for t in range(4):
             team_pass(team_hi[t], 1, t, 1, False, True)
         planes_lo = difference(0, e1_lo)
         hq = [quantise("hq0", interleave("h_bf0", planes_lo, ((0, 128, "vector"),)))]
-        w4q = [quantise("w4q0", prepare_w4(0, ("scalar", "scalar")))]
+        w4_bf0 = prepare_w4(0, ((0, P, "scalar"),))
 
         def out_pass(acc, t, g):
             cols = slice(P * t, P * (t + 1))
             nc.tensor.matmul_mx(out=acc[:], lhsT=w4q[g][0][:, cols].bitcast(FP8X4), lhsT_scale=w4q[g][1][:, cols],
                                 rhs=hq[g][0][:].bitcast(FP8X4), rhs_scale=hq[g][1][:], start=(g == 0), stop=(g == 1))
 
-        y_acc = [bank("low%d" % t, "y%d" % t) for t in range(4)]
-        for t in range(4):
-            out_pass(y_acc[t], t, 0)
         e1_hi = sbuf("e1_hi", [P, 4, S], F32, "w1_raw01")
         for t in range(4):
             nc.scalar.activation(out=e1_hi[:, t, :], in_=team_hi[t][:], func=GELU)
         planes_hi = difference(1, e1_hi)
-        w4_bf1 = prepare_w4(1, ("scalar", "scalar"))
-        h_hi = interleave("h_bf1", planes_hi, ((0, 80, "vector"), (80, 128, "scalar")))
+        w4q = [quantise("w4q0", w4_bf0, "w1_raw01")]
+        y_acc = [bank("low%d" % t, "y%d" % t) for t in range(4)]
+        for t in range(4):
+            out_pass(y_acc[t], t, 0)
+        w4_bf1 = prepare_w4(1, ((0, P, "scalar"),))
+        h_hi = interleave("h_bf1", planes_hi, ((0, 72, "vector"), (72, 128, "scalar")))
         w4q.append(quantise("w4q1", w4_bf1))
         hq.append(quantise("hq1", h_hi))
         y = sbuf("y_sb", [P, 4, S], F32)
@@ -298,9 +311,16 @@ def tile_list_lacrosse_matchup_features_kernel(
         for t in range(4):
             out_pass(y_acc[t], t, 1)
             copy_on("scalar" if t % 2 == 0 else "vector", y[:, t, :], y_acc[t][:])
-            nc.sync.dma_start(out=y_rows[:, t, :], in_=y[:, t, :])
-        y_codes, y_scales = quantise("yq", interleave("y_bf", y, ((0, 80, "vector"), (80, 128, "scalar"))))
-        nc.sync.dma_start(out=out_1[0].rearrange("p m t -> p (m t)").bitcast(I32), in_=y_codes[:].bitcast(I32))
+            if t % 2:
+                nc.sync.dma_start(out=y_rows[:, t - 1 : t + 1, :], in_=y[:, t - 1 : t + 1, :])
+        y_bf = interleave("y_bf", y, ((0, 64, "vector"), (64, 112, "scalar"), (112, 128, "vector")))
+        y_codes = sbuf("y_codes", [P, S], U32)
+        y_scales = sbuf("y_scales", [P, S], U8)
+        y_words = out_1[0].rearrange("p m t -> p (m t)").bitcast(I32)
+        for half in range(2):
+            cols = slice(half * S // 2, (half + 1) * S // 2)
+            nc.vector.quantize_mx(out=y_codes[:, cols].bitcast(FP8X4), scales=y_scales[:, cols], in_=y_bf[:, 2 * S * half : 2 * S * (half + 1)])
+            nc.sync.dma_start(out=y_words[:, cols], in_=y_codes[:, cols].bitcast(I32))
         for r in range(4):
             queue = nc.scalar if r % 2 == 0 else nc.sync
             queue.dma_start(out=out_2[0, r:16:4, :].bitcast(I32), in_=y_scales[r:P:32, :].bitcast(I32))

from contextlib import ExitStack

import concourse.mybir as mybir

K, K3, T, T3, S, H, N = 1024, 512, 2048, 1024, 512, 1024, 512
FLOPS = 2 * S * (2 * K * H + K3 * H + H * N)

F32 = mybir.dt.float32
BF16 = mybir.dt.bfloat16
I32 = mybir.dt.int32
U32 = mybir.dt.uint32
U16 = mybir.dt.uint16
U8 = mybir.dt.uint8
FP8X4 = mybir.dt.float8_e4m3fn_x4
FP4X4 = mybir.dt.float4_e2m1fn_x4
GELU = mybir.ActivationFunctionType.Gelu_apprx_tanh
COPY = mybir.ActivationFunctionType.Copy
ADD = mybir.AluOpType.add
MULT = mybir.AluOpType.mult
SUBTRACT = mybir.AluOpType.subtract

P = 128
G = 512
TAB_ROW = 8
REPEATED = (0, 0, 0, 384)


def tile_list_lacrosse_matchup_features_kernel(
    tc, tab_words, tab_scales, tab2_words, tab2_scales, tab3_words, tab3_scales, offs, offs2, offs3,
    w1, w2_words, w2_scales, w3_words, w3_scales, gain, w4, out_0, out_1, out_2,
):
    nc = tc.nc
    with ExitStack() as ctx:
        lists = ctx.enter_context(tc.tile_pool(name="lists", bufs=1))
        sb = ctx.enter_context(tc.tile_pool(name="sb", bufs=1))
        ps = ctx.enter_context(tc.psum_pool(name="ps", bufs=1))

        def sbuf(name, shape, dtype, tag=""):
            return sb.tile(shape, dtype, name=name, tag=tag or name, align_bytes=64)

        def bank(tag, name):
            return ps.tile([P, S], F32, name=name, tag=tag)

        idx = lists.tile([P, S // 16], U16, name="idx")
        idx2 = lists.tile([P, S // 16], U16, name="idx2")
        idx3 = lists.tile([P, S // 16], U16, name="idx3")

        t3s = sbuf("t3s", [P, T3], U8)
        w3s_raw = sbuf("w3s_raw", [P, H], U8)
        w2s_raw = sbuf("w2s_raw", [P, 2, H], U8)
        t2s = sbuf("t2s", [P, 2, T], U8)
        t1s = sbuf("t1s", [P, T], U8)
        for plane in (t3s[:], w3s_raw[:], w2s_raw[:].rearrange("p a c -> p (a c)")):
            nc.gpsimd.memset(plane.bitcast(I32), 0)
        for plane in (t2s[:].rearrange("p a c -> p (a c)"), t1s[:]):
            nc.vector.memset(plane.bitcast(I32), 0)

        t3w = sbuf("t3w", [P, T3], U16)
        w3w_raw = sbuf("w3w_raw", [P, H], I32)
        w2w_raw = sbuf("w2w_raw", [P, 2, H // 2], I32)
        t2w = [sbuf("t2w%d" % a, [P, T], U32) for a in range(2)]
        t1w = [sbuf("t1w%d" % a, [P, T], U32) for a in range(2)]
        w1_raw = {(g, a): sbuf("w1_raw%d%d" % (g, a), [P, 4, G], F32) for g in range(2) for a in range(2)}
        w4_raw = [sbuf("w4_raw%d" % g, [P, 4, N], F32) for g in range(2)]
        gain_sb = sbuf("gain_sb", [P, 2, 16], F32)

        def load_words(dst, words):
            nc.sync.dma_start(out=dst[:].bitcast(I32), in_=words.rearrange("p t i -> p (t i)").bitcast(I32))

        def load_w1(g, a):
            nc.sync.dma_start(out=w1_raw[g, a][:], in_=w1[G * a : G * (a + 1), G * g : G * (g + 1)].rearrange("(p j) c -> p j c", j=4))

        def load_plane(eng, dst, scales):
            for r in range(4):
                eng.dma_start(out=dst[r:P:32, :].bitcast(I32), in_=scales[0, r:16:4, :].bitcast(I32))

        def load_tab_planes(eng):
            for q in range(4):
                eng.dma_start(
                    out=t1s[32 * q + TAB_ROW : 32 * q + TAB_ROW + 8, :].bitcast(I32),
                    in_=tab_scales[:, 4 * q : 4 * q + 4, :].bitcast(I32),
                )

        def load_two_planes(eng, dst, scales):
            for r in range(4):
                eng.dma_start(out=dst[r:P:32, :, :].bitcast(I32), in_=scales[:, r:16:4, :].rearrange("a q t -> q a t").bitcast(I32))

        def load_gain(eng):
            gain_runs = gain.rearrange("(g u c) -> u g c", g=2, c=16)
            for i in range(4):
                eng.dma_start(out=gain_sb[i:P:4, :, 0:13], in_=gain_runs[:, :, i : i + 13])

        nc.sync.dma_start(idx3[:], offs3)
        nc.sync.dma_start(out=t3w[:].bitcast(I32), in_=tab3_words[0].bitcast(I32))
        load_words(w3w_raw, w3_words[0])
        nc.sync.dma_start(idx2[:], offs2)
        load_plane(nc.sync, t3s, tab3_scales)
        load_words(t2w[0], tab2_words[0])
        load_plane(nc.sync, w3s_raw, w3_scales)
        nc.sync.dma_start(out=w2w_raw[:], in_=w2_words.rearrange("a p c -> p a c").bitcast(I32))
        load_two_planes(nc.sync, t2s, tab2_scales)
        nc.sync.dma_start(idx[:], offs)
        load_words(t2w[1], tab2_words[1])
        load_two_planes(nc.sync, w2s_raw, w2_scales)
        load_w1(0, 0)
        load_tab_planes(nc.sync)
        load_words(t1w[0], tab_words[0])
        load_gain(nc.sync)
        load_w1(0, 1)
        load_words(t1w[1], tab_words[1])
        load_w1(1, 0)
        load_w1(1, 1)
        for g in range(2):
            rows = w4[G * g : G * (g + 1), :].rearrange("(u t i) n -> t u i n", t=4, i=4)
            for t in range(4):
                nc.sync.dma_start(out=w4_raw[g][:, t, :], in_=rows[t])

        def gather(name, window, offsets, dtype, tag=""):
            picked = sbuf(name, [P, S], dtype, tag)
            nc.vector.tensor_copy(picked[:], window.indirect(offsets[:]))
            return picked

        def quantise(name, src, tag=""):
            codes = sbuf(name + "_codes", [P, G], U32, tag)
            scales = sbuf(name + "_scales", [P, G], U8)
            nc.vector.quantize_mx(out=codes[:].bitcast(FP8X4), scales=scales[:], in_=src[:])
            return codes, scales

        def deal_scales(name, raw, groups):
            dealt = sbuf(name, [P, groups * G], U8)
            nc.vector.tensor_copy(
                out=dealt[:].bitcast(I32).rearrange("p (g t u) -> p g t u", t=4, u=32),
                in_=raw.bitcast(I32).rearrange("p (g u t) -> p g t u", t=4, u=32),
            )
            return dealt

        def copy_on(engine, out, in_):
            if engine == "vector":
                nc.vector.tensor_copy(out=out, in_=in_)
            else:
                nc.scalar.copy(out=out, in_=in_)

        def prepare_w1(g, a, engines):
            rounded = sbuf("w1_bf%d%d" % (g, a), [P, 4 * G], BF16, "w1_bf%d" % (2 * g + a))
            dst = rounded[:].rearrange("p (t u i j) -> p t u j i", t=4, i=4, j=4)
            src = w1_raw[g, a][:].rearrange("p j (u t i) -> p t u j i", t=4, i=4)
            for lo, hi, engine in engines:
                copy_on(engine, dst[:, lo:hi], src[:, lo:hi])
            return rounded

        def prepare_w4(g, engines):
            rounded = sbuf("w4_bf%d" % g, [P, 4 * N], BF16)
            dst = rounded[:].rearrange("p (t m j) -> p m j t", t=4, j=4)
            src = w4_raw[g][:].rearrange("p j (m t) -> p m j t", t=4)
            for lo, hi, engine in engines:
                copy_on(engine, dst[:, lo:hi], src[:, lo:hi])
            return rounded

        def interleave(name, planes, shares, tag=""):
            woven = sbuf(name, [P, 4 * S], BF16, tag)
            dst = woven[:].rearrange("p (c i t) -> p c t i", i=4, t=4)
            src = planes[:].rearrange("p t (c i) -> p c t i", i=4)
            for lo, hi, engine in shares:
                copy_on(engine, dst[:, lo:hi], src[:, lo:hi])
            return woven

        v3w = gather("v3w", t3w[:], idx3, U16)
        w3w = sbuf("w3w", [P, H], I32)
        nc.vector.tensor_copy(
            out=w3w[:].rearrange("p (g t u i) -> p g t u i", t=4, u=32, i=4),
            in_=w3w_raw[:].rearrange("p (g u t i) -> p g t u i", t=4, u=32, i=4),
        )
        v3s = gather("v3s", t3s[:], idx3, U8)
        w3s = deal_scales("w3s", w3s_raw[:], 2)
        v2w = [gather("v2w0", t2w[0][:], idx2, U32)]

        def field_pass(acc, g, t, lo, hi, start, stop):
            cols = slice(G * g + P * t, G * g + P * (t + 1))
            nc.tensor.matmul_mx(out=acc[:, lo:hi], lhsT=w3w[:, cols].bitcast(FP8X4), lhsT_scale=w3s[:, cols],
                                rhs=v3w[:, lo:hi].bitcast(FP4X4), rhs_scale=v3s[:, lo:hi], start=start, stop=stop)

        def repeat_field(acc, t):
            for lo in range(0, REPEATED[t], P):
                field_pass(acc, 0, t, lo, lo + P, False, False)

        field = sbuf("field_sb", [P, 4, S], F32)
        for t in range(4):
            acc = bank("low%d" % t, "field%d" % t)
            field_pass(acc, 0, t, REPEATED[t], S, True, True)
            nc.scalar.copy(out=field[:, t, REPEATED[t] : S], in_=acc[:, REPEATED[t] : S])

        def add_field(x, acc):
            for t in range(4):
                nc.vector.tensor_tensor(out=x[:, t, REPEATED[t] : S], in0=acc[t][:, REPEATED[t] : S], in1=field[:, t, REPEATED[t] : S], op=ADD)

        def gelu_low(e, x, acc):
            for t in range(4):
                if REPEATED[t]:
                    nc.scalar.activation(out=e[:, t, 0 : REPEATED[t]], in_=acc[t][:, 0 : REPEATED[t]], func=GELU)
                nc.scalar.activation(out=e[:, t, REPEATED[t] : S], in_=x[:, t, REPEATED[t] : S], func=GELU)

        v2s = [gather("v2s%d" % a, t2s[:, a, :], idx2, U8) for a in range(2)]
        w2w = sbuf("w2w", [P, H], I32)
        nc.vector.tensor_copy(
            out=w2w[:].rearrange("p (b t u e) -> p b t u e", t=4, u=32, e=2),
            in_=w2w_raw[:].rearrange("p a c -> p (a c)").rearrange("p (b u t e) -> p b t u e", t=4, u=32, e=2),
        )
        w2s = deal_scales("w2s", w2s_raw[:].rearrange("p a c -> p (a c)"), 4)
        v2w.append(gather("v2w1", t2w[1][:], idx2, U32))

        def opp_pass(acc, g, t, a, start, stop):
            c0 = H * a + G * g + P * t
            nc.tensor.matmul_mx(out=acc[:], lhsT=w2w[:, c0 // 2 : (c0 + P) // 2].bitcast(FP4X4), lhsT_scale=w2s[:, c0 : c0 + P],
                                rhs=v2w[a][:].bitcast(FP8X4), rhs_scale=v2s[a][:], start=start, stop=stop)

        def gain_of(g, t):
            return gain_sb[:, g, 4 * t : 4 * t + 1]

        opp_hi = [bank("high%d" % t, "opp_hi%d" % t) for t in range(4)]
        opp_lo = [bank("low%d" % t, "opp_lo%d" % t) for t in range(4)]
        for t in range(4):
            field_pass(opp_hi[t], 1, t, 0, S, True, False)
        for t in range(4):
            opp_pass(opp_lo[t], 0, t, 0, True, False)
            repeat_field(opp_lo[t], t)
            opp_pass(opp_lo[t], 0, t, 1, False, True)
        for t in range(4):
            opp_pass(opp_hi[t], 1, t, 1, False, False)
            opp_pass(opp_hi[t], 1, t, 0, False, True)

        w1_bf = {(0, 0): prepare_w1(0, 0, ((0, 4, "scalar"),))}
        x2 = sbuf("x2", [P, 4, S], F32, "x")
        add_field(x2, opp_lo)
        e2 = [sbuf("e2_lo", [P, 4, S], F32, "w1_raw00"), sbuf("e2_hi", [P, 4, S], F32, "w1_bf0")]
        gelu_low(e2[0], x2, opp_lo)
        w1q = {(0, 0): quantise("w1q00", w1_bf[0, 0])}
        for t in range(4):
            nc.scalar.activation(out=e2[1][:, t, :], in_=opp_hi[t][:], func=GELU)

        team_hi = [bank("high%d" % t, "team_hi%d" % t) for t in range(4)]
        v1s = gather("v1s", t1s[:], idx, U8)
        v1w = [gather("v1w0", t1w[0][:], idx, U32)]

        def team_pass(acc, g, t, a, start, stop):
            codes, scales = w1q[g, a]
            cols = slice(P * t, P * (t + 1))
            nc.tensor.matmul_mx(out=acc[:], lhsT=codes[:, cols].bitcast(FP8X4), lhsT_scale=scales[:, cols],
                                rhs=v1w[a][:].bitcast(FP8X4), rhs_scale=v1s[TAB_ROW + 4 * a : P, :], start=start, stop=stop)

        team_lo = [bank("low%d" % t, "team_lo%d" % t) for t in range(4)]
        for t in range(4):
            team_pass(team_lo[t], 0, t, 0, True, False)
            repeat_field(team_lo[t], t)
        for t in range(4):
            field_pass(team_hi[t], 1, t, 0, S, True, False)

        w1_bf[0, 1] = prepare_w1(0, 1, ((0, 4, "vector"),))
        w1q[0, 1] = quantise("w1q01", w1_bf[0, 1])
        e2g = [e2[0]]
        for t in range(4):
            nc.scalar.activation(out=e2g[0][:, t, :], in_=e2[0][:, t, :], func=COPY, scale=gain_of(0, t))
        v1w.append(gather("v1w1", t1w[1][:], idx, U32))
        e2g.append(sbuf("e2g_hi", [P, 4, S], F32, "t1w1"))
        for t in range(2):
            nc.vector.tensor_scalar(out=e2g[1][:, t, :], in0=e2[1][:, t, :], scalar1=gain_of(1, t), scalar2=None, op0=MULT)
            nc.scalar.activation(out=e2g[1][:, 2 + t, :], in_=e2[1][:, 2 + t, :], func=COPY, scale=gain_of(1, 2 + t))
        for t in range(4):
            team_pass(team_lo[t], 0, t, 1, False, True)

        def difference(g, e1):
            planes = sbuf("h_planes%d" % g, [P, 4, S], BF16)
            for t in range(4):
                nc.vector.scalar_tensor_tensor(out=planes[:, t, :], in0=e1[:, t, :], scalar=gain_of(g, t), in1=e2g[g][:, t, :], op0=MULT, op1=SUBTRACT)
            return planes

        x1 = sbuf("x1", [P, 4, S], F32, "x")
        add_field(x1, team_lo)
        w1_bf[1, 0] = prepare_w1(1, 0, ((0, 3, "scalar"), (3, 4, "vector")))
        w1q[1, 0] = quantise("w1q10", w1_bf[1, 0])
        for t in range(4):
            team_pass(team_hi[t], 1, t, 0, False, False)
        e1_lo = sbuf("e1_lo", [P, 4, S], F32, "w1_raw10")
        gelu_low(e1_lo, x1, team_lo)
        w1_bf[1, 1] = prepare_w1(1, 1, ((0, 4, "vector"),))
        w1q[1, 1] = quantise("w1q11", w1_bf[1, 1])
        for t in range(4):
            team_pass(team_hi[t], 1, t, 1, False, True)
        planes_lo = difference(0, e1_lo)
        hq = [quantise("hq0", interleave("h_bf0", planes_lo, ((0, 128, "vector"),)))]
        w4_bf0 = prepare_w4(0, ((0, P, "scalar"),))

        def out_pass(acc, t, g):
            cols = slice(P * t, P * (t + 1))
            nc.tensor.matmul_mx(out=acc[:], lhsT=w4q[g][0][:, cols].bitcast(FP8X4), lhsT_scale=w4q[g][1][:, cols],
                                rhs=hq[g][0][:].bitcast(FP8X4), rhs_scale=hq[g][1][:], start=(g == 0), stop=(g == 1))

        e1_hi = sbuf("e1_hi", [P, 4, S], F32, "w1_raw01")
        for t in range(4):
            nc.scalar.activation(out=e1_hi[:, t, :], in_=team_hi[t][:], func=GELU)
        planes_hi = difference(1, e1_hi)
        w4q = [quantise("w4q0", w4_bf0, "w1_raw01")]
        y_acc = [bank("low%d" % t, "y%d" % t) for t in range(4)]
        for t in range(4):
            out_pass(y_acc[t], t, 0)
        w4_bf1 = prepare_w4(1, ((0, P, "scalar"),))
        h_hi = interleave("h_bf1", planes_hi, ((0, 72, "vector"), (72, 128, "scalar")))
        w4q.append(quantise("w4q1", w4_bf1))
        hq.append(quantise("hq1", h_hi))
        y = sbuf("y_sb", [P, 4, S], F32)
        y_rows = out_0.rearrange("(p t) s -> p t s", t=4)
        for t in range(4):
            out_pass(y_acc[t], t, 1)
            copy_on("scalar" if t % 2 == 0 else "vector", y[:, t, :], y_acc[t][:])
            if t % 2:
                nc.sync.dma_start(out=y_rows[:, t - 1 : t + 1, :], in_=y[:, t - 1 : t + 1, :])
        y_bf = interleave("y_bf", y, ((0, 64, "vector"), (64, 112, "scalar"), (112, 128, "vector")))
        y_codes = sbuf("y_codes", [P, S], U32)
        y_scales = sbuf("y_scales", [P, S], U8)
        y_words = out_1[0].rearrange("p m t -> p (m t)").bitcast(I32)
        for half in range(2):
            cols = slice(half * S // 2, (half + 1) * S // 2)
            nc.vector.quantize_mx(out=y_codes[:, cols].bitcast(FP8X4), scales=y_scales[:, cols], in_=y_bf[:, 2 * S * half : 2 * S * (half + 1)])
            nc.sync.dma_start(out=y_words[:, cols], in_=y_codes[:, cols].bitcast(I32))
        for r in range(4):
            queue = nc.scalar if r % 2 == 0 else nc.sync
            queue.dma_start(out=out_2[0, r:16:4, :].bitcast(I32), in_=y_scales[r:P:32, :].bitcast(I32))
